import numpy as np
CORES = [114,242,370,498]
N = 4
ROOT = 3
def setup_inputs(rng):
    return {"x": rng.standard_normal((N, 128, 256), dtype=np.float32)}
def reference(x):
    y = np.full((N, 128, N * 256), np.nan, x.dtype)
    y[ROOT] = np.concatenate(list(x), axis=1)
    return {"y": y}

@@ -1,0 +1,59 @@
+from concourse.bass import RemoteDMATransfer, DstId
+G = 16
+NG = 128 // G
+SCRATCH = {'l0': ('dram', [NG, 128, 2 * G], 'float32'), 'l1': ('dram', [NG, 128, 2 * G], 'float32'), 'l2': ('dram', [128, 256], 'float32')}
+SEMAPHORES = ['ld', 'st', 'sent', 'b0', 'q0', 'q1', 'q2', 'q3', 'q4', 'q5', 'q6', 'q7', 'q8', 'q9']
+R0, R1, R2, ROOT = (114, 242, 370, 498)
+H01, H45, H67 = (R0 - 2, R0 + 2, R0 + 4)
+RA = R2 + 4
+WAYS = [(0, 0, 2, None), (0, 2, 2, H67), (0, 4, 2, H45), (0, 6, 2, H01), (1, 0, 3, RA), (1, 3, 2, R0), (1, 5, 1, H67), (1, 6, 1, H45), (1, 7, 1, H01)]
+FIRST = {0: 2, 1: 1}
+STORES = [([0, 1, 2, 3], 0, 0, 8), ([4, 5, 6, 7, 8], 1, 0, 8)]
+
+def share(n):
+    return {1: 8, 2: 4, 3: 2, 4: 2}.get(n, 1)
+
+def rank_program(g, core, T, topo):
+    q = [T.sem.q0, T.sem.q1, T.sem.q2, T.sem.q3, T.sem.q4, T.sem.q5, T.sem.q6, T.sem.q7, T.sem.q8, T.sem.q9]
+    img = [T.l0, T.l1]
+
+    def transfers(ways, to_root, per):
+        out, e = ([], 0)
+        for i in ways:
+            rank, g0, ng, relay = WAYS[i]
+            rid, pid = topo.addr(ROOT if to_root or relay is None else relay, core)
+            for k in range(g0, g0 + ng):
+                out.append(RemoteDMATransfer(dst_ids=[DstId(rid=rid, pnc=pid)], dma_engine_mask=(1 << per) - 1 << e, remote_sem=q[i], src=img[rank][k], dst=img[rank][k]))
+                e += per
+        return out
+    sent = 0
+    if core == R2:
+        rid, pid = topo.addr(ROOT, core)
+        g.dma_start(T.l2[:, :], T.x[:, :]).then_inc(T.sem.ld, 16)
+        g.wait_ge(T.sem.ld, 16)
+        g.remote_dma(T.l2[:, :], T.l2[:, :], T.sem.b0, T.sem.sent, pid, rid, 255)
+        sent += 8
+    if core == R0 or core == R1:
+        rank = 0 if core == R0 else 1
+        mine = [i for i, w in enumerate(WAYS) if w[0] == rank]
+        g.dma_start(img[rank][0:NG], T.x[:, :]).then_inc(T.sem.ld, 16)
+        g.wait_ge(T.sem.ld, 16)
+        g.remote_dma_fused(transfers(mine, False, FIRST[rank]), local_sem=T.sem.sent)
+        sent += FIRST[rank] * NG
+    for i, w in enumerate(WAYS):
+        if w[3] == core:
+            g.wait_ge(q[i], FIRST[w[0]] * w[2])
+            g.remote_dma_fused(transfers([i], True, share(w[2])), local_sem=T.sem.sent)
+            sent += share(w[2]) * w[2]
+    if sent:
+        g.wait_ge(T.sem.sent, sent)
+    if core == ROOT:
+        g.dma_start(T.y[:, 768:1024], T.x[:, :]).then_inc(T.sem.st, 16)
+        g.wait_ge(T.sem.b0, 8)
+        g.dma_start(T.y[:, 512:768], T.l2[:, :]).then_inc(T.sem.st, 16)
+        for ways, rank, g0, ng in STORES:
+            for i in ways:
+                w = WAYS[i]
+                g.wait_ge(q[i], (FIRST[w[0]] if w[3] is None else share(w[2])) * w[2])
+            g.dma_start(T.y[g0 * G:(g0 + ng) * G, 256 * rank:256 * rank + 256], img[rank][g0:g0 + ng]).then_inc(T.sem.st, 16)
+        g.wait_ge(T.sem.st, 16 * (2 + len(STORES)))

@@ -2,16 +2,19 @@ from concourse.bass import RemoteDMATransfer, DstId
 G = 16
 NG = 128 // G
 SCRATCH = {'l0': ('dram', [NG, 128, 2 * G], 'float32'), 'l1': ('dram', [NG, 128, 2 * G], 'float32'), 'l2': ('dram', [128, 256], 'float32')}
-SEMAPHORES = ['ld', 'st', 'sent', 'b0', 'q0', 'q1', 'q2', 'q3', 'q4', 'q5', 'q6', 'q7', 'q8', 'q9']
+SEMAPHORES = ['ld', 'st', 'sh', 'sent', 'b0', 'q0', 'q1', 'q2', 'q3', 'q4', 'q5', 'q6', 'q7', 'q8', 'q9']
 R0, R1, R2, ROOT = (114, 242, 370, 498)
 H01, H45, H67 = (R0 - 2, R0 + 2, R0 + 4)
 RA = R2 + 4
 WAYS = [(0, 0, 2, None), (0, 2, 2, H67), (0, 4, 2, H45), (0, 6, 2, H01), (1, 0, 3, RA), (1, 3, 2, R0), (1, 5, 1, H67), (1, 6, 1, H45), (1, 7, 1, H01)]
 FIRST = {0: 2, 1: 1}
-STORES = [([0, 1, 2, 3], 0, 0, 8), ([4, 5, 6, 7, 8], 1, 0, 8)]
+STORES = [(0, [0], 0, 0, 2), (0, [1, 2, 3], 0, 2, 6), (0, [5], 1, 3, 2),
+          (1, [4], 1, 0, 3), (1, [6, 7, 8], 1, 5, 3)]
+
 
 def share(n):
     return {1: 8, 2: 4, 3: 2, 4: 2}.get(n, 1)
+
 
 def rank_program(g, core, T, topo):
     q = [T.sem.q0, T.sem.q1, T.sem.q2, T.sem.q3, T.sem.q4, T.sem.q5, T.sem.q6, T.sem.q7, T.sem.q8, T.sem.q9]
@@ -29,14 +32,14 @@ def rank_program(g, core, T, topo):
     sent = 0
     if core == R2:
         rid, pid = topo.addr(ROOT, core)
-        g.dma_start(T.l2[:, :], T.x[:, :]).then_inc(T.sem.ld, 16)
+        g.sync.dma_start(T.l2[:, :], T.x[:, :]).then_inc(T.sem.ld, 16)
         g.wait_ge(T.sem.ld, 16)
         g.remote_dma(T.l2[:, :], T.l2[:, :], T.sem.b0, T.sem.sent, pid, rid, 255)
         sent += 8
     if core == R0 or core == R1:
         rank = 0 if core == R0 else 1
         mine = [i for i, w in enumerate(WAYS) if w[0] == rank]
-        g.dma_start(img[rank][0:NG], T.x[:, :]).then_inc(T.sem.ld, 16)
+        g.sync.dma_start(img[rank][0:NG], T.x[:, :]).then_inc(T.sem.ld, 16)
         g.wait_ge(T.sem.ld, 16)
         g.remote_dma_fused(transfers(mine, False, FIRST[rank]), local_sem=T.sem.sent)
         sent += FIRST[rank] * NG
@@ -48,12 +51,14 @@ def rank_program(g, core, T, topo):
     if sent:
         g.wait_ge(T.sem.sent, sent)
     if core == ROOT:
+        qs = [g.sync, g.scalar]
         g.dma_start(T.y[:, 768:1024], T.x[:, :]).then_inc(T.sem.st, 16)
-        g.wait_ge(T.sem.b0, 8)
-        g.dma_start(T.y[:, 512:768], T.l2[:, :]).then_inc(T.sem.st, 16)
-        for ways, rank, g0, ng in STORES:
+        g.scalar.wait_ge(T.sem.b0, 8)
+        g.scalar.dma_start(T.y[:, 512:768], T.l2[:, :]).then_inc(T.sem.sh, 16)
+        for qi, ways, rank, g0, ng in STORES:
             for i in ways:
                 w = WAYS[i]
-                g.wait_ge(q[i], (FIRST[w[0]] if w[3] is None else share(w[2])) * w[2])
-            g.dma_start(T.y[g0 * G:(g0 + ng) * G, 256 * rank:256 * rank + 256], img[rank][g0:g0 + ng]).then_inc(T.sem.st, 16)
-        g.wait_ge(T.sem.st, 16 * (2 + len(STORES)))
+                qs[qi].wait_ge(q[i], (FIRST[w[0]] if w[3] is None else share(w[2])) * w[2])
+            qs[qi].dma_start(T.y[g0 * G:(g0 + ng) * G, 256 * rank:256 * rank + 256], img[rank][g0:g0 + ng]).then_inc(T.sem.sh, 16)
+        g.wait_ge(T.sem.st, 16)
+        g.wait_ge(T.sem.sh, 16 * (1 + len(STORES)))

@@ -1,15 +1,22 @@
 from concourse.bass import RemoteDMATransfer, DstId
-G = 16
-NG = 128 // G
-SCRATCH = {'l0': ('dram', [NG, 128, 2 * G], 'float32'), 'l1': ('dram', [NG, 128, 2 * G], 'float32'), 'l2': ('dram', [128, 256], 'float32')}
-SEMAPHORES = ['ld', 'st', 'sh', 'sent', 'b0', 'q0', 'q1', 'q2', 'q3', 'q4', 'q5', 'q6', 'q7', 'q8', 'q9']
+U = 8
+NU = 128 // U
+SCRATCH = {'l0': ('dram', [NU, 128, 2 * U], 'float32'), 'l1': ('dram', [NU, 128, 2 * U], 'float32'), 'l2': ('dram', [NU, 128, 2 * U], 'float32')}
 R0, R1, R2, ROOT = (114, 242, 370, 498)
-H01, H45, H67 = (R0 - 2, R0 + 2, R0 + 4)
-RA = R2 + 4
-WAYS = [(0, 0, 2, None), (0, 2, 2, H67), (0, 4, 2, H45), (0, 6, 2, H01), (1, 0, 3, RA), (1, 3, 2, R0), (1, 5, 1, H67), (1, 6, 1, H45), (1, 7, 1, H01)]
-FIRST = {0: 2, 1: 1}
-STORES = [(0, [0], 0, 0, 2), (0, [1, 2, 3], 0, 2, 6), (0, [5], 1, 3, 2),
-          (1, [4], 1, 0, 3), (1, [6, 7, 8], 1, 5, 3)]
+B0, B2 = 112, 368
+WAYS = [
+    (0, 0, 4, None, 0), (0, 4, 4, B0 + 6, 0), (0, 8, 4, B0 + 4, 0), (0, 12, 4, B0 + 0, 0),
+    (1, 0, 3, B2 + 6, 0), (1, 3, 2, B0 + 3, 0), (1, 5, 1, B0 + 7, 0), (1, 6, 1, B0 + 5, 0), (1, 7, 1, B0 + 1, 0),
+    (1, 8, 3, B2 + 7, 1), (1, 11, 2, R0, 1), (1, 13, 1, B0 + 6, 1), (1, 14, 1, B0 + 4, 1), (1, 15, 1, B0 + 0, 1),
+    (2, 0, 8, None, 0), (2, 8, 8, None, 1),
+]
+CHUNKS = {R0: (0, [(0, 16)]), R1: (1, [(0, 8), (8, 8)]), R2: (2, [(0, 8), (8, 8)])}
+STORES = [
+    (2, [0], 0, 0, 4),
+    (0, [1, 2, 3], 0, 4, 12), (0, [5, 6, 7, 8], 1, 3, 5), (0, [10, 11, 12, 13], 1, 11, 5),
+    (1, [14], 2, 0, 8), (1, [4], 1, 0, 3), (1, [15], 2, 8, 8), (1, [9], 1, 8, 3),
+]
+SEMAPHORES = ['lda', 'ldb', 'st', 'sh', 'sent'] + ['q%d' % i for i in range(len(WAYS))]
 
 
 def share(n):
@@ -17,48 +24,47 @@ def share(n):
 
 
 def rank_program(g, core, T, topo):
-    q = [T.sem.q0, T.sem.q1, T.sem.q2, T.sem.q3, T.sem.q4, T.sem.q5, T.sem.q6, T.sem.q7, T.sem.q8, T.sem.q9]
-    img = [T.l0, T.l1]
+    q = [T.sem.q0, T.sem.q1, T.sem.q2, T.sem.q3, T.sem.q4, T.sem.q5, T.sem.q6, T.sem.q7, T.sem.q8, T.sem.q9, T.sem.q10, T.sem.q11, T.sem.q12, T.sem.q13, T.sem.q14, T.sem.q15]
+    img = [T.l0, T.l1, T.l2]
 
     def transfers(ways, to_root, per):
         out, e = ([], 0)
         for i in ways:
-            rank, g0, ng, relay = WAYS[i]
+            rank, u0, nu, relay, _ = WAYS[i]
             rid, pid = topo.addr(ROOT if to_root or relay is None else relay, core)
-            for k in range(g0, g0 + ng):
+            for k in range(u0, u0 + nu):
                 out.append(RemoteDMATransfer(dst_ids=[DstId(rid=rid, pnc=pid)], dma_engine_mask=(1 << per) - 1 << e, remote_sem=q[i], src=img[rank][k], dst=img[rank][k]))
                 e += per
         return out
     sent = 0
-    if core == R2:
-        rid, pid = topo.addr(ROOT, core)
-        g.sync.dma_start(T.l2[:, :], T.x[:, :]).then_inc(T.sem.ld, 16)
-        g.wait_ge(T.sem.ld, 16)
-        g.remote_dma(T.l2[:, :], T.l2[:, :], T.sem.b0, T.sem.sent, pid, rid, 255)
-        sent += 8
-    if core == R0 or core == R1:
-        rank = 0 if core == R0 else 1
-        mine = [i for i, w in enumerate(WAYS) if w[0] == rank]
-        g.sync.dma_start(img[rank][0:NG], T.x[:, :]).then_inc(T.sem.ld, 16)
-        g.wait_ge(T.sem.ld, 16)
-        g.remote_dma_fused(transfers(mine, False, FIRST[rank]), local_sem=T.sem.sent)
-        sent += FIRST[rank] * NG
+    if core in CHUNKS:
+        rank, chunks = CHUNKS[core]
+        lq = [g.sync, g.scalar]
+        ls = [T.sem.lda, T.sem.ldb]
+        for c, (u0, nu) in enumerate(chunks):
+            lq[c].dma_start(img[rank][u0:u0 + nu], T.x[u0 * U:(u0 + nu) * U, :]).then_inc(ls[c], 16)
+        for c, (u0, nu) in enumerate(chunks):
+            mine = [i for i, w in enumerate(WAYS) if w[0] == rank and w[4] == c]
+            g.wait_ge(ls[c], 16)
+            g.remote_dma_fused(transfers(mine, False, 1), local_sem=T.sem.sent)
+            sent += nu
     for i, w in enumerate(WAYS):
         if w[3] == core:
-            g.wait_ge(q[i], FIRST[w[0]] * w[2])
+            g.wait_ge(q[i], w[2])
             g.remote_dma_fused(transfers([i], True, share(w[2])), local_sem=T.sem.sent)
             sent += share(w[2]) * w[2]
     if sent:
         g.wait_ge(T.sem.sent, sent)
     if core == ROOT:
-        qs = [g.sync, g.scalar]
+        qs = [g.sync, g.scalar, g]
+        ss = [T.sem.sh, T.sem.sh, T.sem.st]
+        n = [0, 0, 1]
         g.dma_start(T.y[:, 768:1024], T.x[:, :]).then_inc(T.sem.st, 16)
-        g.scalar.wait_ge(T.sem.b0, 8)
-        g.scalar.dma_start(T.y[:, 512:768], T.l2[:, :]).then_inc(T.sem.sh, 16)
-        for qi, ways, rank, g0, ng in STORES:
+        for qi, ways, rank, u0, nu in STORES:
             for i in ways:
                 w = WAYS[i]
-                qs[qi].wait_ge(q[i], (FIRST[w[0]] if w[3] is None else share(w[2])) * w[2])
-            qs[qi].dma_start(T.y[g0 * G:(g0 + ng) * G, 256 * rank:256 * rank + 256], img[rank][g0:g0 + ng]).then_inc(T.sem.sh, 16)
-        g.wait_ge(T.sem.st, 16)
-        g.wait_ge(T.sem.sh, 16 * (1 + len(STORES)))
+                qs[qi].wait_ge(q[i], (1 if w[3] is None else share(w[2])) * w[2])
+            qs[qi].dma_start(T.y[u0 * U:(u0 + nu) * U, 256 * rank:256 * rank + 256], img[rank][u0:u0 + nu]).then_inc(ss[qi], 16)
+            n[qi] += 1
+        g.wait_ge(T.sem.st, 16 * n[2])
+        g.wait_ge(T.sem.sh, 16 * (n[0] + n[1]))

@@ -1,22 +1,21 @@
 from concourse.bass import RemoteDMATransfer, DstId
-U = 8
-NU = 128 // U
-SCRATCH = {'l0': ('dram', [NU, 128, 2 * U], 'float32'), 'l1': ('dram', [NU, 128, 2 * U], 'float32'), 'l2': ('dram', [NU, 128, 2 * U], 'float32')}
+UR = [16, 8, 64]
+PER = [2, 1, 8]
+SCRATCH = {'l0': ('dram', [128 // UR[0], 128, 2 * UR[0]], 'float32'), 'l1': ('dram', [128 // UR[1], 128, 2 * UR[1]], 'float32'), 'l2': ('dram', [128 // UR[2], 128, 2 * UR[2]], 'float32')}
 R0, R1, R2, ROOT = (114, 242, 370, 498)
 B0, B2 = 112, 368
 WAYS = [
-    (0, 0, 4, None, 0), (0, 4, 4, B0 + 6, 0), (0, 8, 4, B0 + 4, 0), (0, 12, 4, B0 + 0, 0),
-    (1, 0, 3, B2 + 6, 0), (1, 3, 2, B0 + 3, 0), (1, 5, 1, B0 + 7, 0), (1, 6, 1, B0 + 5, 0), (1, 7, 1, B0 + 1, 0),
-    (1, 8, 3, B2 + 7, 1), (1, 11, 2, R0, 1), (1, 13, 1, B0 + 6, 1), (1, 14, 1, B0 + 4, 1), (1, 15, 1, B0 + 0, 1),
-    (2, 0, 8, None, 0), (2, 8, 8, None, 1),
+    (0, 0, 2, None, 0), (0, 2, 2, B0 + 6, 0), (0, 4, 2, B0 + 4, 0), (0, 6, 2, B0 + 0, 0),
+    (1, 0, 3, B2 + 1, 0), (1, 3, 2, B0 + 3, 0), (1, 5, 1, B0 + 7, 0), (1, 6, 1, B0 + 5, 0), (1, 7, 1, B0 + 1, 0),
+    (1, 8, 3, B2 + 3, 1), (1, 11, 2, R0, 1), (1, 13, 1, B0 + 6, 1), (1, 14, 1, B0 + 4, 1), (1, 15, 1, B0 + 0, 1),
+    (2, 0, 1, None, 0), (2, 1, 1, B2 + 4, 0),
 ]
-CHUNKS = {R0: (0, [(0, 16)]), R1: (1, [(0, 8), (8, 8)]), R2: (2, [(0, 8), (8, 8)])}
+CHUNKS = {R0: (0, [(0, 8)]), R1: (1, [(0, 8), (8, 8)]), R2: (2, [(0, 2)])}
 STORES = [
-    (2, [0], 0, 0, 4),
-    (0, [1, 2, 3], 0, 4, 12), (0, [5, 6, 7, 8], 1, 3, 5), (0, [10, 11, 12, 13], 1, 11, 5),
-    (1, [14], 2, 0, 8), (1, [4], 1, 0, 3), (1, [15], 2, 8, 8), (1, [9], 1, 8, 3),
+    (0, [0], 0, 0, 2), (0, [1, 2, 3], 0, 2, 6), (0, [5, 6, 7, 8], 1, 3, 5), (0, [10, 11, 12, 13], 1, 11, 5),
+    (1, [14], 2, 0, 1), (1, [4], 1, 0, 3), (1, [15], 2, 1, 1), (1, [9], 1, 8, 3),
 ]
-SEMAPHORES = ['lda', 'ldb', 'st', 'sh', 'sent'] + ['q%d' % i for i in range(len(WAYS))]
+SEMAPHORES = ['lda', 'ldb', 'st', 'sh', 'sent'] + ['q%d' % i for i in range(16)]
 
 
 def share(n):
@@ -39,6 +38,7 @@ def rank_program(g, core, T, topo):
     sent = 0
     if core in CHUNKS:
         rank, chunks = CHUNKS[core]
+        U = UR[rank]
         lq = [g.sync, g.scalar]
         ls = [T.sem.lda, T.sem.ldb]
         for c, (u0, nu) in enumerate(chunks):
@@ -46,11 +46,11 @@ def rank_program(g, core, T, topo):
         for c, (u0, nu) in enumerate(chunks):
             mine = [i for i, w in enumerate(WAYS) if w[0] == rank and w[4] == c]
             g.wait_ge(ls[c], 16)
-            g.remote_dma_fused(transfers(mine, False, 1), local_sem=T.sem.sent)
-            sent += nu
+            g.remote_dma_fused(transfers(mine, False, PER[rank]), local_sem=T.sem.sent)
+            sent += nu * PER[rank]
     for i, w in enumerate(WAYS):
         if w[3] == core:
-            g.wait_ge(q[i], w[2])
+            g.wait_ge(q[i], w[2] * PER[w[0]])
             g.remote_dma_fused(transfers([i], True, share(w[2])), local_sem=T.sem.sent)
             sent += share(w[2]) * w[2]
     if sent:
@@ -61,9 +61,10 @@ def rank_program(g, core, T, topo):
         n = [0, 0, 1]
         g.dma_start(T.y[:, 768:1024], T.x[:, :]).then_inc(T.sem.st, 16)
         for qi, ways, rank, u0, nu in STORES:
+            U = UR[rank]
             for i in ways:
                 w = WAYS[i]
-                qs[qi].wait_ge(q[i], (1 if w[3] is None else share(w[2])) * w[2])
+                qs[qi].wait_ge(q[i], (PER[w[0]] if w[3] is None else share(w[2])) * w[2])
             qs[qi].dma_start(T.y[u0 * U:(u0 + nu) * U, 256 * rank:256 * rank + 256], img[rank][u0:u0 + nu]).then_inc(ss[qi], 16)
             n[qi] += 1
         g.wait_ge(T.sem.st, 16 * n[2])

@@ -1,19 +1,19 @@
 from concourse.bass import RemoteDMATransfer, DstId
-UR = [16, 8, 64]
-PER = [2, 1, 8]
+UR = [32, 16, 64]
+PER = [4, 2, 8]
 SCRATCH = {'l0': ('dram', [128 // UR[0], 128, 2 * UR[0]], 'float32'), 'l1': ('dram', [128 // UR[1], 128, 2 * UR[1]], 'float32'), 'l2': ('dram', [128 // UR[2], 128, 2 * UR[2]], 'float32')}
 R0, R1, R2, ROOT = (114, 242, 370, 498)
 B0, B2 = 112, 368
 WAYS = [
-    (0, 0, 2, None, 0), (0, 2, 2, B0 + 6, 0), (0, 4, 2, B0 + 4, 0), (0, 6, 2, B0 + 0, 0),
-    (1, 0, 3, B2 + 1, 0), (1, 3, 2, B0 + 3, 0), (1, 5, 1, B0 + 7, 0), (1, 6, 1, B0 + 5, 0), (1, 7, 1, B0 + 1, 0),
-    (1, 8, 3, B2 + 3, 1), (1, 11, 2, R0, 1), (1, 13, 1, B0 + 6, 1), (1, 14, 1, B0 + 4, 1), (1, 15, 1, B0 + 0, 1),
+    (0, 0, 1, None, 0), (0, 1, 1, B0 + 6, 0), (0, 2, 1, B0 + 4, 0), (0, 3, 1, B0 + 0, 0),
+    (1, 0, 1, B2 + 1, 0), (1, 1, 1, B0 + 3, 0), (1, 2, 1, B0 + 7, 0), (1, 3, 1, B0 + 5, 0),
+    (1, 4, 1, B2 + 3, 1), (1, 5, 1, B2 + 0, 1), (1, 6, 1, B0 + 1, 1), (1, 7, 1, R0, 1),
     (2, 0, 1, None, 0), (2, 1, 1, B2 + 4, 0),
 ]
-CHUNKS = {R0: (0, [(0, 8)]), R1: (1, [(0, 8), (8, 8)]), R2: (2, [(0, 2)])}
+CHUNKS = {R0: (0, [(0, 4)]), R1: (1, [(0, 4), (4, 4)]), R2: (2, [(0, 2)])}
 STORES = [
-    (0, [0], 0, 0, 2), (0, [1, 2, 3], 0, 2, 6), (0, [5, 6, 7, 8], 1, 3, 5), (0, [10, 11, 12, 13], 1, 11, 5),
-    (1, [14], 2, 0, 1), (1, [4], 1, 0, 3), (1, [15], 2, 1, 1), (1, [9], 1, 8, 3),
+    (0, [0], 0, 0, 1), (0, [1, 2, 3], 0, 1, 3), (0, [5, 6, 7], 1, 1, 3), (0, [10, 11], 1, 6, 2),
+    (1, [12], 2, 0, 1), (1, [4], 1, 0, 1), (1, [13], 2, 1, 1), (1, [8, 9], 1, 4, 2),
 ]
 SEMAPHORES = ['lda', 'ldb', 'st', 'sh', 'sent'] + ['q%d' % i for i in range(16)]
 

from concourse.bass import RemoteDMATransfer, DstId
UR = [32, 16, 64]
PER = [4, 2, 8]
SCRATCH = {'l0': ('dram', [128 // UR[0], 128, 2 * UR[0]], 'float32'), 'l1': ('dram', [128 // UR[1], 128, 2 * UR[1]], 'float32'), 'l2': ('dram', [128 // UR[2], 128, 2 * UR[2]], 'float32')}
R0, R1, R2, ROOT = (114, 242, 370, 498)
B0, B2 = 112, 368
WAYS = [
    (0, 0, 1, None, 0), (0, 1, 1, B0 + 6, 0), (0, 2, 1, B0 + 4, 0), (0, 3, 1, B0 + 0, 0),
    (1, 0, 1, B2 + 1, 0), (1, 1, 1, B0 + 3, 0), (1, 2, 1, B0 + 7, 0), (1, 3, 1, B0 + 5, 0),
    (1, 4, 1, B2 + 3, 1), (1, 5, 1, B2 + 0, 1), (1, 6, 1, B0 + 1, 1), (1, 7, 1, R0, 1),
    (2, 0, 1, None, 0), (2, 1, 1, B2 + 4, 0),
]
CHUNKS = {R0: (0, [(0, 4)]), R1: (1, [(0, 4), (4, 4)]), R2: (2, [(0, 2)])}
STORES = [
    (0, [0], 0, 0, 1), (0, [1, 2, 3], 0, 1, 3), (0, [5, 6, 7], 1, 1, 3), (0, [10, 11], 1, 6, 2),
    (1, [12], 2, 0, 1), (1, [4], 1, 0, 1), (1, [13], 2, 1, 1), (1, [8, 9], 1, 4, 2),
]
SEMAPHORES = ['lda', 'ldb', 'st', 'sh', 'sent'] + ['q%d' % i for i in range(16)]


def share(n):
    return {1: 8, 2: 4, 3: 2, 4: 2}.get(n, 1)


def rank_program(g, core, T, topo):
    q = [T.sem.q0, T.sem.q1, T.sem.q2, T.sem.q3, T.sem.q4, T.sem.q5, T.sem.q6, T.sem.q7, T.sem.q8, T.sem.q9, T.sem.q10, T.sem.q11, T.sem.q12, T.sem.q13, T.sem.q14, T.sem.q15]
    img = [T.l0, T.l1, T.l2]

    def transfers(ways, to_root, per):
        out, e = ([], 0)
        for i in ways:
            rank, u0, nu, relay, _ = WAYS[i]
            rid, pid = topo.addr(ROOT if to_root or relay is None else relay, core)
            for k in range(u0, u0 + nu):
                out.append(RemoteDMATransfer(dst_ids=[DstId(rid=rid, pnc=pid)], dma_engine_mask=(1 << per) - 1 << e, remote_sem=q[i], src=img[rank][k], dst=img[rank][k]))
                e += per
        return out
    sent = 0
    if core in CHUNKS:
        rank, chunks = CHUNKS[core]
        U = UR[rank]
        lq = [g.sync, g.scalar]
        ls = [T.sem.lda, T.sem.ldb]
        for c, (u0, nu) in enumerate(chunks):
            lq[c].dma_start(img[rank][u0:u0 + nu], T.x[u0 * U:(u0 + nu) * U, :]).then_inc(ls[c], 16)
        for c, (u0, nu) in enumerate(chunks):
            mine = [i for i, w in enumerate(WAYS) if w[0] == rank and w[4] == c]
            g.wait_ge(ls[c], 16)
            g.remote_dma_fused(transfers(mine, False, PER[rank]), local_sem=T.sem.sent)
            sent += nu * PER[rank]
    for i, w in enumerate(WAYS):
        if w[3] == core:
            g.wait_ge(q[i], w[2] * PER[w[0]])
            g.remote_dma_fused(transfers([i], True, share(w[2])), local_sem=T.sem.sent)
            sent += share(w[2]) * w[2]
    if sent:
        g.wait_ge(T.sem.sent, sent)
    if core == ROOT:
        qs = [g.sync, g.scalar, g]
        ss = [T.sem.sh, T.sem.sh, T.sem.st]
        n = [0, 0, 1]
        g.dma_start(T.y[:, 768:1024], T.x[:, :]).then_inc(T.sem.st, 16)
        for qi, ways, rank, u0, nu in STORES:
            U = UR[rank]
            for i in ways:
                w = WAYS[i]
                qs[qi].wait_ge(q[i], (PER[w[0]] if w[3] is None else share(w[2])) * w[2])
            qs[qi].dma_start(T.y[u0 * U:(u0 + nu) * U, 256 * rank:256 * rank + 256], img[rank][u0:u0 + nu]).then_inc(ss[qi], 16)
            n[qi] += 1
        g.wait_ge(T.sem.st, 16 * n[2])
        g.wait_ge(T.sem.sh, 16 * (n[0] + n[1]))
